import numpy as np
import ml_dtypes


def mxq(x, axis, fmt="e4m3"):
    dtype, down = {"e4m3": (ml_dtypes.float8_e4m3fn, 7), "e5m2": (ml_dtypes.float8_e5m2, 14)}[fmt]
    v = np.moveaxis(np.asarray(x, np.float32).astype(ml_dtypes.bfloat16).astype(np.float64), axis, -1)
    blocks = v.reshape(v.shape[:-1] + (-1, 32))
    amax = np.abs(blocks).max(-1, keepdims=True)
    byte = np.maximum(np.where(amax > 0, np.frexp(amax)[1] - 1 + 127, 0) - down, 1)
    scale = np.exp2(byte - 127.0)
    codes = (blocks / scale).astype(np.float32).astype(dtype).astype(np.float64)
    return np.moveaxis((codes * scale).reshape(v.shape), -1, axis)


WIDE = False


def mx_kscale(k):
    if not WIDE:
        return np.ones(k)
    levels = np.array([10, -10, 5, -5, 0])
    if k % 512:
        return np.exp2(np.random.permutation(np.resize(levels, k // 32))).repeat(32)
    a = np.empty((k // 512, 16))
    for p in range(k // 512):
        a[p, :8] = np.random.permutation(np.resize(levels, 8))
        for g in range(8):
            far = levels[np.abs(levels - a[p, g]) >= 10]
            a[p, g + 8] = far[np.random.randint(len(far))]
    return np.exp2(a.ravel()).repeat(32)


def f64(x):
    return np.asarray(x).astype(np.float64)


def striped(idx):
    return np.tile(idx.reshape(-1, 16).T, (8, 1)).astype(np.uint16)


def unstriped(offs):
    return offs[:16].T.reshape(-1).astype(np.int64)


def striped8(idx):
    return np.concatenate([x.reshape(-1, 16).T for x in idx]).astype(np.uint16)


def runs(offs, k):
    lists = np.stack([offs[16 * r : 16 * r + 16].T.reshape(-1) for r in range(8)]).astype(np.int64)
    return lists[np.arange(k) % 512 // 64]


def pack_weight(w):
    k, n = w.shape
    w = f64(np.asarray(w, np.float32).astype(ml_dtypes.bfloat16)).reshape(k // 32, 32, n)
    amax = np.abs(w).max(1)
    byte = np.clip(np.where(amax > 0, np.frexp(amax)[1] - 1 + 127 - 7, 1), 1, 254)
    scaled = (w * np.exp2(127.0 - byte)[:, None, :]).reshape(k, n).astype(np.float32)
    words = np.ascontiguousarray(scaled.reshape(k // 512, 128, 4, n).transpose(0, 1, 3, 2)).astype(ml_dtypes.float8_e4m3fn).view(np.uint8)
    return words, np.ascontiguousarray(byte.astype(np.uint8).reshape(k // 512, 16, n))


def unpack_weight(words, scales):
    g, p, n, _ = words.shape
    vals = np.ascontiguousarray(words).view(ml_dtypes.float8_e4m3fn).astype(np.float64) * np.repeat(np.exp2(scales.astype(np.float64) - 127.0), 8, axis=1)[..., None]
    return vals.transpose(0, 1, 3, 2).reshape(g * 512, n)


E2M1 = np.array([0.0, 0.5, 1.0, 1.5, 2.0, 3.0, 4.0, 6.0, -0.0, -0.5, -1.0, -1.5, -2.0, -3.0, -4.0, -6.0])


def pack_fp4(w):
    k, n = w.shape
    w = f64(np.asarray(w, np.float32).astype(ml_dtypes.bfloat16)).reshape(k // 32, 32, n)
    amax = np.abs(w).max(1)
    mant, ex = np.frexp(amax / 6.0)
    byte = np.clip(np.where(amax > 0, np.where(mant > 0.5, ex, ex - 1) + 127, 1), 1, 254)
    scaled = (w * np.exp2(127.0 - byte)[:, None, :]).reshape(k, n).astype(np.float32)
    c = np.ascontiguousarray(scaled.reshape(k // 512, 128, 4, n).transpose(0, 1, 3, 2)).astype(ml_dtypes.float4_e2m1fn).view(np.uint8) & 0xF
    words = (c[..., 0::2] | (c[..., 1::2] << 4)).reshape(k // 512, 128, 2 * n)
    return np.ascontiguousarray(words), np.ascontiguousarray(byte.astype(np.uint8).reshape(k // 512, 16, n))


def unpack_fp4(words, scales):
    g, _, n = scales.shape
    words = np.ascontiguousarray(words).reshape(g, 128, n, 2)
    nib = np.empty((g, 128, n, 4), np.uint8)
    nib[..., 0::2] = words & 0xF
    nib[..., 1::2] = words >> 4
    vals = E2M1[nib] * np.repeat(np.exp2(scales.astype(np.float64) - 127.0), 8, axis=1)[..., None]
    return vals.transpose(0, 1, 3, 2).reshape(g * 512, n)


def planes(y):
    n, m = y.shape
    v = y.astype(np.float32).astype(ml_dtypes.bfloat16).astype(np.float64).reshape(n // 32, 32, m)
    top = np.abs(v).max(1)
    byte = np.clip(np.where(top > 0, np.frexp(top)[1] - 1 + 127 - 7, 1), 1, 254)
    codes = (v * np.exp2(127.0 - byte)[:, None, :]).reshape(n, m).astype(np.float32).astype(ml_dtypes.float8_e4m3fn).view(np.uint8)
    words = codes.reshape(n // 512, 128, 4, m).transpose(0, 1, 3, 2)
    return np.ascontiguousarray(words), np.ascontiguousarray(byte.astype(np.uint8).reshape(n // 512, 16, m))


K, T, S, N, G, H = 512, 2048, 512, 512, 2048, 512


def setup_inputs():
    n = np.random.standard_normal
    s = mx_kscale(K)[:, None]
    u = mx_kscale(S)
    packed_xT = pack_weight(n((K, T)) * s)
    packed_dT = pack_weight(n((K, G)) / s)
    packed_w1 = pack_fp4(n((H, N)) / np.sqrt(H) / u[:, None])
    return {
        "x_words": packed_xT[0],
        "x_scales": packed_xT[1],
        "d_words": packed_dT[0],
        "d_scales": packed_dT[1],
        "gn": (np.random.uniform(0.5, 1.5, (H, 1)) * u[:, None]).astype(np.float32),
        "w1_words": packed_w1[0],
        "w1_scales": packed_w1[1],
        "offs": striped8(np.random.randint(0, T, (8, S))),
        "k1": striped8(np.random.randint(0, G, (8, H))),
        "n1": striped(np.random.permutation(S)),
        "n2": striped(np.random.permutation(S)),
        "n3": striped(np.random.permutation(S)),
        "n4": striped(np.random.permutation(S)),
    }


def reference(x_words, x_scales, d_words, d_scales, gn, w1_words, w1_scales, offs, k1, n1, n2, n3, n4):
    d_k1 = unpack_weight(d_words, d_scales)[np.arange(K)[:, None], runs(k1, K)]
    xq = unpack_weight(x_words, x_scales)[np.arange(K)[:, None], runs(offs, K)]
    h = 0.0625 * (d_k1.T @ xq)
    st = h - h[:, unstriped(n1)]
    z = f64(gn) * (np.maximum(st, st[:, unstriped(n2)]))
    h2 = unpack_fp4(w1_words, w1_scales).T @ mxq(z, 0, "e4m3")
    out_0 = h2[:, unstriped(n3)] + 0.75 * h2[:, unstriped(n4)]
    return (out_0,) + planes(out_0)

@@ -1,0 +1,217 @@
+from contextlib import ExitStack
+
+import concourse.mybir as mybir
+
+K, T, S, N, G, H = 512, 2048, 512, 512, 2048, 512
+FLOPS = 2 * K * H * S + 2 * H * N * S
+
+F32 = mybir.dt.float32
+BF16 = mybir.dt.bfloat16
+I32 = mybir.dt.int32
+U32 = mybir.dt.uint32
+U16 = mybir.dt.uint16
+U8 = mybir.dt.uint8
+FP8X4 = mybir.dt.float8_e4m3fn_x4
+FP4X4 = mybir.dt.float4_e2m1fn_x4
+ACT = mybir.ActivationFunctionType
+ALU = mybir.AluOpType
+
+P = 128
+HALF = S // 2
+CHUNK = 128
+Z_CHUNKS = [(j0, CHUNK) for j0 in range(0, S, CHUNK)]
+OUT_CHUNKS = [(j0, CHUNK) for j0 in range(0, S, CHUNK)]
+N1_ON_VECTOR = (0, 1)
+
+
+def entries(lst, j0, n):
+    return lst[:, j0 // 16 : (j0 + n) // 16]
+
+
+def tile_picked_hpqhopmxsum_none_po_kernel(
+    tc, x_words, x_scales, d_words, d_scales, gn, w1_words, w1_scales, offs, k1, n1, n2, n3, n4, out_0, out_1, out_2
+):
+    nc = tc.nc
+    with ExitStack() as ctx:
+        lists = ctx.enter_context(tc.tile_pool(name="lists", bufs=1))
+        sb = ctx.enter_context(tc.tile_pool(name="sb", bufs=1))
+        psum = ctx.enter_context(tc.psum_pool(name="psum", bufs=1))
+
+        def load_list(name, src):
+            lst = lists.tile([P, S // 16], U16, name=name)
+            nc.sync.dma_start(lst[:], src)
+            return lst
+
+        def words_of(packed):
+            return packed[0].rearrange("p n r -> p (n r)").bitcast(I32)
+
+        gain = sb.tile([P, 4], F32)
+        nc.scalar.dma_start(gain[:], gn.rearrange("(p t) o -> p (t o)", t=4))
+
+        k1_l = load_list("k1_l", k1)
+        offs_l = load_list("offs_l", offs)
+
+        d_scale_tab = sb.tile([P, G], U8, align_bytes=64)
+        x_scale_tab = sb.tile([P, T], U8, tag="x_scale_then_w1_raw", align_bytes=64)
+        nc.vector.memset(d_scale_tab[:].bitcast(I32), 0)
+        nc.gpsimd.memset(x_scale_tab[:].bitcast(I32), 0)
+        nc.scalar.dma_start(d_scale_tab[0:P:8, :].bitcast(I32), d_scales[0].bitcast(I32))
+        nc.scalar.dma_start(x_scale_tab[0:P:8, :].bitcast(I32), x_scales[0].bitcast(I32))
+
+        d_tab = sb.tile([P, G], I32, align_bytes=64)
+        nc.sync.dma_start(d_tab[:], words_of(d_words))
+        n1_l = load_list("n1_l", n1)
+        n2_l = load_list("n2_l", n2)
+        n3_l = load_list("n3_l", n3)
+        n4_l = load_list("n4_l", n4)
+        x_tab = sb.tile([P, T], I32, tag="x_words_then_w1_dealt", align_bytes=64)
+        nc.sync.dma_start(x_tab[:], words_of(x_words))
+
+        planes = sb.tile([P, S + H], U8, align_bytes=64)
+        nc.vector.memset(planes[:].bitcast(I32), 0)
+
+        gain_abs = sb.tile([P, 4], F32)
+        nc.scalar.activation(gain_abs[:], gain[:], ACT.Abs, scale=0.0625)
+        widest = max(n for j0, n in Z_CHUNKS)
+        gain_sign = sb.tile([P, widest, 4], BF16, align_bytes=64)
+        nc.scalar.activation(gain_sign[:], gain[:].unsqueeze(1).to_broadcast([P, widest, 4]), ACT.Sign)
+
+        picked_scales = sb.tile([P, S + H], U8, align_bytes=64)
+        nc.vector.tensor_copy(picked_scales[:, S:], d_scale_tab[:].indirect(k1_l[:]))
+        nc.vector.tensor_copy(picked_scales[:, :S], x_scale_tab[:].indirect(offs_l[:]))
+        for q in range(4):
+            nc.scalar.dma_start(
+                planes[32 * q : 32 * q + 4, :].bitcast(I32), picked_scales[32 * q : 32 * q + 32 : 8, :].bitcast(I32)
+            )
+
+        w1_raw = sb.tile([P, 3 * N], U8, tag="x_scale_then_w1_raw", align_bytes=64)
+        nc.gpsimd.memset(w1_raw[:, 2 * N :].bitcast(I32), 0)
+        nc.sync.dma_start(w1_raw[:, : 2 * N].bitcast(I32), w1_words[0].bitcast(I32))
+        for q in range(4):
+            nc.sync.dma_start(
+                w1_raw[32 * q : 32 * q + 4, 2 * N :].bitcast(I32), w1_scales[0, 4 * q : 4 * q + 4, :].bitcast(I32)
+            )
+
+        d_picked = sb.tile([P, H], U32, align_bytes=64)
+        nc.vector.tensor_copy(d_picked[:], d_tab[:].bitcast(U32).indirect(k1_l[:]))
+        d_codes = sb.tile([P, H], U32, align_bytes=64)
+        nc.vector.tensor_copy(
+            d_codes[:].bitcast(I32).rearrange("p (t c i) -> p c t i", t=4, i=4),
+            d_picked[:].bitcast(I32).rearrange("p (c i t) -> p c t i", t=4, i=4),
+        )
+        d_plane = sb.tile([P, H], U8, align_bytes=64)
+        nc.vector.tensor_copy(
+            d_plane[:].rearrange("p (t m) -> p t m", t=4), planes[:, S:].rearrange("p (m t) -> p t m", t=4)
+        )
+
+        x_codes = [sb.tile([P, HALF], U32, name=f"x_codes{u}", align_bytes=64) for u in range(2)]
+        for u in range(2):
+            nc.vector.tensor_copy(x_codes[u][:], x_tab[:].bitcast(U32).indirect(entries(offs_l, u * HALF, HALF)))
+
+        w1_dealt = sb.tile([P, 3 * N], U8, tag="x_words_then_w1_dealt", align_bytes=64)
+        nc.vector.tensor_copy(
+            w1_dealt[:, : 2 * N].rearrange("p (t m b) -> p t m b", t=4, b=2),
+            w1_raw[:, : 2 * N].rearrange("p (m t b) -> p t m b", t=4, b=2),
+        )
+        nc.vector.tensor_copy(
+            w1_dealt[:, 2 * N :].rearrange("p (t m) -> p t m", t=4),
+            w1_raw[:, 2 * N :].rearrange("p (m t) -> p t m", t=4),
+        )
+
+        h = [sb.tile([P, S], F32, name=f"h{t}") for t in range(4)]
+        for t, u in [(t, u) for pair in range(2) for u in range(2) for t in (2 * pair, 2 * pair + 1)]:
+            acc = psum.tile([P, HALF], F32, name="acc", tag=f"bank{2 * t + u}")
+            nc.tensor.matmul_mx(
+                out=acc[:],
+                lhsT=d_codes[:, t * P : (t + 1) * P].bitcast(FP8X4),
+                lhsT_scale=d_plane[:, t * P : (t + 1) * P],
+                rhs=x_codes[u][:].bitcast(FP8X4),
+                rhs_scale=planes[:, u * HALF : (u + 1) * HALF],
+                start=True,
+                stop=True,
+            )
+            nc.scalar.activation(h[t][:, u * HALF : (u + 1) * HALF], acc[:], ACT.Copy, scale=gain_abs[:, t : t + 1])
+
+        st = sb.tile([P, 4, S], F32)
+        for t in range(4):
+            h_n1 = sb.tile([P, S], F32, name=f"h_n1_{t}")
+            for u in range(2):
+                window = h[t][:].indirect(entries(n1_l, u * HALF, HALF))
+                if t in N1_ON_VECTOR:
+                    nc.vector.tensor_copy(h_n1[:, u * HALF : (u + 1) * HALF], window)
+                else:
+                    nc.scalar.activation(h_n1[:, u * HALF : (u + 1) * HALF], window, ACT.Copy)
+            nc.vector.tensor_tensor(st[:, t, :], h[t][:], h_n1[:], ALU.subtract)
+
+        st_n2 = [sb.tile([P, 4, CHUNK], F32, name=f"st_n2_{c}") for c in range(4)]
+        for c, (j0, n) in enumerate(Z_CHUNKS):
+            for t in range(4):
+                window = st[:, t, :].indirect(entries(n2_l, j0, n))
+                if c == 0 and t >= 2:
+                    nc.vector.tensor_copy(st_n2[c][:, t, :], window)
+                else:
+                    nc.scalar.activation(st_n2[c][:, t, :], window, ACT.Copy)
+
+        early = [psum.tile([P, 2 * CHUNK], F32, name="early", tag=f"bank{t}") for t in range(4)]
+        late = [psum.tile([P, 2, CHUNK], F32, name="late", tag=f"bank{4 + b}") for b in range(4)]
+        for c, (j0, n) in enumerate(Z_CHUNKS):
+            z_abs = sb.tile([P, 4 * n], BF16, name=f"z_abs{c}", align_bytes=64)
+            nc.vector.tensor_tensor(
+                z_abs[:].rearrange("p (c i t) -> p c t i", t=4, i=4),
+                st[:, :, j0 : j0 + n].rearrange("p t (c i) -> p c t i", i=4),
+                st_n2[c][:].rearrange("p t (c i) -> p c t i", i=4),
+                ALU.max,
+            )
+            z = sb.tile([P, 4 * n], BF16, name=f"z{c}", align_bytes=64)
+            nc.vector.tensor_tensor(z[:], z_abs[:], gain_sign[:, :n, :].rearrange("p j t -> p (j t)"), ALU.mult)
+            z_codes = sb.tile([P, n], U32, name=f"z_codes{c}", align_bytes=64)
+            z_plane = sb.tile([P, n], U8, name=f"z_plane{c}", align_bytes=64)
+            nc.vector.quantize_mx(out=z_codes[:].bitcast(FP8X4), scales=z_plane[:], in_=z[:])
+            for t in range(4):
+                nc.tensor.matmul_mx(
+                    out=early[t][:, j0 : j0 + n] if c < 2 else late[2 * (c - 2) + t // 2][:, t % 2, :],
+                    lhsT=w1_dealt[:, 2 * t * P : 2 * (t + 1) * P].bitcast(FP4X4),
+                    lhsT_scale=w1_dealt[:, 2 * N + t * P : 2 * N + (t + 1) * P],
+                    rhs=z_codes[:].bitcast(FP8X4),
+                    rhs_scale=z_plane[:],
+                    start=True,
+                    stop=True,
+                )
+
+        h2 = [sb.tile([P, S], F32, name=f"h2_{t}") for t in range(4)]
+        for t in range(4):
+            nc.scalar.copy(h2[t][:, : 2 * CHUNK], early[t][:])
+        for c in (2, 3):
+            for t in range(4):
+                src = late[2 * (c - 2) + t // 2][:, t % 2, :]
+                if c == 3 and t >= 2:
+                    nc.vector.tensor_copy(h2[t][:, c * CHUNK : (c + 1) * CHUNK], src)
+                else:
+                    nc.scalar.copy(h2[t][:, c * CHUNK : (c + 1) * CHUNK], src)
+
+        out_rows = out_0.rearrange("(p t) j -> p t j", t=4)
+        out_codes = sb.tile([P, S], U32, align_bytes=64)
+        out_plane = sb.tile([P, S], U8, align_bytes=64)
+        for c, (j0, n) in enumerate(OUT_CHUNKS):
+            h2_n4 = sb.tile([P, 4, n], F32, name=f"h2_n4_{c}")
+            y = sb.tile([P, 4, n], F32, name=f"y{c}")
+            for t in range(4):
+                nc.scalar.activation(h2_n4[:, t, :], h2[t][:].indirect(entries(n4_l, j0, n)), ACT.Copy, scale=0.75)
+                if t == 3 and c < 3:
+                    h2_n3 = sb.tile([P, n], F32, name=f"h2_n3_{c}")
+                    nc.scalar.activation(h2_n3[:], h2[t][:].indirect(entries(n3_l, j0, n)), ACT.Copy)
+                    nc.vector.tensor_tensor(y[:, t, :], h2_n3[:], h2_n4[:, t, :], ALU.add)
+                else:
+                    nc.vector.tensor_tensor(y[:, t, :], h2[t][:].indirect(entries(n3_l, j0, n)), h2_n4[:, t, :], ALU.add)
+            nc.sync.dma_start(out_rows[:, :, j0 : j0 + n], y[:])
+            y_bf = sb.tile([P, 4 * n], BF16, name=f"y_bf{c}", align_bytes=64)
+            nc.vector.tensor_copy(
+                y_bf[:].rearrange("p (c i t) -> p c t i", t=4, i=4), y[:].rearrange("p t (c i) -> p c t i", i=4)
+            )
+            nc.vector.quantize_mx(
+                out=out_codes[:, j0 : j0 + n].bitcast(FP8X4), scales=out_plane[:, j0 : j0 + n], in_=y_bf[:]
+            )
+            nc.sync.dma_start(words_of(out_1)[:, j0 : j0 + n], out_codes[:, j0 : j0 + n].bitcast(I32))
+        for q in range(4):
+            queue = nc.scalar if q % 2 else nc.sync
+            queue.dma_start(out_2[0, 4 * q : 4 * q + 4, :].bitcast(I32), out_plane[32 * q : 32 * q + 4, :].bitcast(I32))

@@ -19,9 +19,9 @@ ALU = mybir.AluOpType
 P = 128
 HALF = S // 2
 CHUNK = 128
+N1_ON_VECTOR = 4
 Z_CHUNKS = [(j0, CHUNK) for j0 in range(0, S, CHUNK)]
-OUT_CHUNKS = [(j0, CHUNK) for j0 in range(0, S, CHUNK)]
-N1_ON_VECTOR = (0, 1)
+OUT_CHUNKS = [(0, 128), (128, 256), (384, 128)]
 
 
 def entries(lst, j0, n):
@@ -45,52 +45,49 @@ def tile_picked_hpqhopmxsum_none_po_kernel(
         def words_of(packed):
             return packed[0].rearrange("p n r -> p (n r)").bitcast(I32)
 
-        gain = sb.tile([P, 4], F32)
-        nc.scalar.dma_start(gain[:], gn.rearrange("(p t) o -> p (t o)", t=4))
-
         k1_l = load_list("k1_l", k1)
         offs_l = load_list("offs_l", offs)
+        gain = sb.tile([P, 4], F32)
+        nc.sync.dma_start(gain[:], gn.rearrange("(p t) o -> p (t o)", t=4))
+        n1_l = load_list("n1_l", n1)
+        n2_l = load_list("n2_l", n2)
+
+        planes = sb.tile([P, S + H + N], U8, align_bytes=64)
+        nc.gpsimd.memset(planes[:, S + H :].bitcast(I32), 0)
+        nc.scalar.dma_start(planes[0:P:8, S + H :].bitcast(I32), w1_scales[0].bitcast(I32))
 
         d_scale_tab = sb.tile([P, G], U8, align_bytes=64)
-        x_scale_tab = sb.tile([P, T], U8, tag="x_scale_then_w1_raw", align_bytes=64)
+        x_scale_tab = sb.tile([P, T], U8, align_bytes=64)
         nc.vector.memset(d_scale_tab[:].bitcast(I32), 0)
         nc.gpsimd.memset(x_scale_tab[:].bitcast(I32), 0)
-        nc.scalar.dma_start(d_scale_tab[0:P:8, :].bitcast(I32), d_scales[0].bitcast(I32))
-        nc.scalar.dma_start(x_scale_tab[0:P:8, :].bitcast(I32), x_scales[0].bitcast(I32))
+        nc.sync.dma_start(d_scale_tab[0:P:8, :].bitcast(I32), d_scales[0].bitcast(I32))
+        nc.sync.dma_start(x_scale_tab[0:P:8, :].bitcast(I32), x_scales[0].bitcast(I32))
 
         d_tab = sb.tile([P, G], I32, align_bytes=64)
         nc.sync.dma_start(d_tab[:], words_of(d_words))
-        n1_l = load_list("n1_l", n1)
-        n2_l = load_list("n2_l", n2)
-        n3_l = load_list("n3_l", n3)
-        n4_l = load_list("n4_l", n4)
         x_tab = sb.tile([P, T], I32, tag="x_words_then_w1_dealt", align_bytes=64)
         nc.sync.dma_start(x_tab[:], words_of(x_words))
-
-        planes = sb.tile([P, S + H], U8, align_bytes=64)
-        nc.vector.memset(planes[:].bitcast(I32), 0)
+        w1_raw = sb.tile([P, 2 * N], U8, align_bytes=64)
+        nc.sync.dma_start(w1_raw[:].bitcast(I32), w1_words[0].bitcast(I32))
+        n3_l = load_list("n3_l", n3)
+        n4_l = load_list("n4_l", n4)
 
         gain_abs = sb.tile([P, 4], F32)
         nc.scalar.activation(gain_abs[:], gain[:], ACT.Abs, scale=0.0625)
-        widest = max(n for j0, n in Z_CHUNKS)
+        widest = CHUNK
         gain_sign = sb.tile([P, widest, 4], BF16, align_bytes=64)
         nc.scalar.activation(gain_sign[:], gain[:].unsqueeze(1).to_broadcast([P, widest, 4]), ACT.Sign)
 
-        picked_scales = sb.tile([P, S + H], U8, align_bytes=64)
-        nc.vector.tensor_copy(picked_scales[:, S:], d_scale_tab[:].indirect(k1_l[:]))
-        nc.vector.tensor_copy(picked_scales[:, :S], x_scale_tab[:].indirect(offs_l[:]))
-        for q in range(4):
-            nc.scalar.dma_start(
-                planes[32 * q : 32 * q + 4, :].bitcast(I32), picked_scales[32 * q : 32 * q + 32 : 8, :].bitcast(I32)
-            )
-
-        w1_raw = sb.tile([P, 3 * N], U8, tag="x_scale_then_w1_raw", align_bytes=64)
-        nc.gpsimd.memset(w1_raw[:, 2 * N :].bitcast(I32), 0)
-        nc.sync.dma_start(w1_raw[:, : 2 * N].bitcast(I32), w1_words[0].bitcast(I32))
-        for q in range(4):
-            nc.sync.dma_start(
-                w1_raw[32 * q : 32 * q + 4, 2 * N :].bitcast(I32), w1_scales[0, 4 * q : 4 * q + 4, :].bitcast(I32)
-            )
+        d_scale_picked = sb.tile([P, H], U8, align_bytes=64)
+        x_scale_picked = sb.tile([P, S], U8, align_bytes=64)
+        nc.vector.tensor_copy(d_scale_picked[:], d_scale_tab[:].indirect(k1_l[:]))
+        nc.vector.tensor_copy(x_scale_picked[:], x_scale_tab[:].indirect(offs_l[:]))
+        nc.vector.tensor_copy(
+            planes[:, S : S + H].rearrange("p (t m) -> p t m", t=4), d_scale_picked[:].rearrange("p (m t) -> p t m", t=4)
+        )
+        nc.vector.tensor_copy(planes[:, :S].bitcast(I32), x_scale_picked[:].bitcast(I32))
+        for r in range(1, 4):
+            nc.scalar.dma_start(planes[r:P:32, :].bitcast(I32), planes[8 * r : P : 32, :].bitcast(I32))
 
         d_picked = sb.tile([P, H], U32, align_bytes=64)
         nc.vector.tensor_copy(d_picked[:], d_tab[:].bitcast(U32).indirect(k1_l[:]))
@@ -98,10 +95,6 @@ def tile_picked_hpqhopmxsum_none_po_kernel(
         nc.vector.tensor_copy(
             d_codes[:].bitcast(I32).rearrange("p (t c i) -> p c t i", t=4, i=4),
             d_picked[:].bitcast(I32).rearrange("p (c i t) -> p c t i", t=4, i=4),
-        )
-        d_plane = sb.tile([P, H], U8, align_bytes=64)
-        nc.vector.tensor_copy(
-            d_plane[:].rearrange("p (t m) -> p t m", t=4), planes[:, S:].rearrange("p (m t) -> p t m", t=4)
         )
 
         x_codes = [sb.tile([P, HALF], U32, name=f"x_codes{u}", align_bytes=64) for u in range(2)]
@@ -111,20 +104,20 @@ def tile_picked_hpqhopmxsum_none_po_kernel(
         w1_dealt = sb.tile([P, 3 * N], U8, tag="x_words_then_w1_dealt", align_bytes=64)
         nc.vector.tensor_copy(
             w1_dealt[:, : 2 * N].rearrange("p (t m b) -> p t m b", t=4, b=2),
-            w1_raw[:, : 2 * N].rearrange("p (m t b) -> p t m b", t=4, b=2),
+            w1_raw[:].rearrange("p (m t b) -> p t m b", t=4, b=2),
         )
         nc.vector.tensor_copy(
             w1_dealt[:, 2 * N :].rearrange("p (t m) -> p t m", t=4),
-            w1_raw[:, 2 * N :].rearrange("p (m t) -> p t m", t=4),
+            planes[:, S + H :].rearrange("p (m t) -> p t m", t=4),
         )
 
         h = [sb.tile([P, S], F32, name=f"h{t}") for t in range(4)]
-        for t, u in [(t, u) for pair in range(2) for u in range(2) for t in (2 * pair, 2 * pair + 1)]:
+        for t, u in [(t, u) for t in range(4) for u in range(2)]:
             acc = psum.tile([P, HALF], F32, name="acc", tag=f"bank{2 * t + u}")
             nc.tensor.matmul_mx(
                 out=acc[:],
                 lhsT=d_codes[:, t * P : (t + 1) * P].bitcast(FP8X4),
-                lhsT_scale=d_plane[:, t * P : (t + 1) * P],
+                lhsT_scale=planes[:, S + t * P : S + (t + 1) * P],
                 rhs=x_codes[u][:].bitcast(FP8X4),
                 rhs_scale=planes[:, u * HALF : (u + 1) * HALF],
                 start=True,
@@ -134,32 +127,33 @@ def tile_picked_hpqhopmxsum_none_po_kernel(
 
         st = sb.tile([P, 4, S], F32)
         for t in range(4):
-            h_n1 = sb.tile([P, S], F32, name=f"h_n1_{t}")
+            h_n1 = [sb.tile([P, HALF], F32, name=f"h_n1_{u}", tag=f"h_n1_{u}" if 2 * t + u < N1_ON_VECTOR else f"h_n1_{t}_{u}") for u in range(2)]
             for u in range(2):
                 window = h[t][:].indirect(entries(n1_l, u * HALF, HALF))
-                if t in N1_ON_VECTOR:
-                    nc.vector.tensor_copy(h_n1[:, u * HALF : (u + 1) * HALF], window)
+                if 2 * t + u < N1_ON_VECTOR:
+                    nc.vector.tensor_copy(h_n1[u][:], window)
                 else:
-                    nc.scalar.activation(h_n1[:, u * HALF : (u + 1) * HALF], window, ACT.Copy)
-            nc.vector.tensor_tensor(st[:, t, :], h[t][:], h_n1[:], ALU.subtract)
+                    nc.scalar.activation(h_n1[u][:], window, ACT.Copy)
+            for u in range(2):
+                cols = slice(u * HALF, (u + 1) * HALF)
+                nc.vector.tensor_tensor(st[:, t, cols], h[t][:, cols], h_n1[u][:], ALU.subtract)
 
         st_n2 = [sb.tile([P, 4, CHUNK], F32, name=f"st_n2_{c}") for c in range(4)]
-        for c, (j0, n) in enumerate(Z_CHUNKS):
-            for t in range(4):
-                window = st[:, t, :].indirect(entries(n2_l, j0, n))
-                if c == 0 and t >= 2:
-                    nc.vector.tensor_copy(st_n2[c][:, t, :], window)
-                else:
-                    nc.scalar.activation(st_n2[c][:, t, :], window, ACT.Copy)
+        for c, t in [(c, t) for c in range(4) for t in range(4)]:
+            window = st[:, t, :].indirect(entries(n2_l, c * CHUNK, CHUNK))
+            if c == 0 and t >= 2:
+                nc.vector.tensor_copy(st_n2[c][:, t, :], window)
+            else:
+                nc.scalar.activation(st_n2[c][:, t, :], window, ACT.Copy)
 
         early = [psum.tile([P, 2 * CHUNK], F32, name="early", tag=f"bank{t}") for t in range(4)]
         late = [psum.tile([P, 2, CHUNK], F32, name="late", tag=f"bank{4 + b}") for b in range(4)]
         for c, (j0, n) in enumerate(Z_CHUNKS):
             z_abs = sb.tile([P, 4 * n], BF16, name=f"z_abs{c}", align_bytes=64)
             nc.vector.tensor_tensor(
-                z_abs[:].rearrange("p (c i t) -> p c t i", t=4, i=4),
-                st[:, :, j0 : j0 + n].rearrange("p t (c i) -> p c t i", i=4),
-                st_n2[c][:].rearrange("p t (c i) -> p c t i", i=4),
+                z_abs[:].rearrange("p (c i t) -> p c t i", t=4, i=2),
+                st[:, :, j0 : j0 + n].rearrange("p t (c i) -> p c t i", i=2),
+                st_n2[c][:].rearrange("p t (c i) -> p c t i", i=2),
                 ALU.max,
             )
             z = sb.tile([P, 4 * n], BF16, name=f"z{c}", align_bytes=64)
@@ -184,7 +178,7 @@ def tile_picked_hpqhopmxsum_none_po_kernel(
         for c in (2, 3):
             for t in range(4):
                 src = late[2 * (c - 2) + t // 2][:, t % 2, :]
-                if c == 3 and t >= 2:
+                if c == 3:
                     nc.vector.tensor_copy(h2[t][:, c * CHUNK : (c + 1) * CHUNK], src)
                 else:
                     nc.scalar.copy(h2[t][:, c * CHUNK : (c + 1) * CHUNK], src)
@@ -197,8 +191,8 @@ def tile_picked_hpqhopmxsum_none_po_kernel(
             y = sb.tile([P, 4, n], F32, name=f"y{c}")
             for t in range(4):
                 nc.scalar.activation(h2_n4[:, t, :], h2[t][:].indirect(entries(n4_l, j0, n)), ACT.Copy, scale=0.75)
-                if t == 3 and c < 3:
-                    h2_n3 = sb.tile([P, n], F32, name=f"h2_n3_{c}")
+                if c == 2 and t >= 1:
+                    h2_n3 = sb.tile([P, n], F32, name=f"h2_n3_{t}")
                     nc.scalar.activation(h2_n3[:], h2[t][:].indirect(entries(n3_l, j0, n)), ACT.Copy)
                     nc.vector.tensor_tensor(y[:, t, :], h2_n3[:], h2_n4[:, t, :], ALU.add)
                 else:
@@ -206,7 +200,7 @@ def tile_picked_hpqhopmxsum_none_po_kernel(
             nc.sync.dma_start(out_rows[:, :, j0 : j0 + n], y[:])
             y_bf = sb.tile([P, 4 * n], BF16, name=f"y_bf{c}", align_bytes=64)
             nc.vector.tensor_copy(
-                y_bf[:].rearrange("p (c i t) -> p c t i", t=4, i=4), y[:].rearrange("p t (c i) -> p c t i", i=4)
+                y_bf[:].rearrange("p (c i t) -> p c t i", t=4, i=2), y[:].rearrange("p t (c i) -> p c t i", i=2)
             )
             nc.vector.quantize_mx(
                 out=out_codes[:, j0 : j0 + n].bitcast(FP8X4), scales=out_plane[:, j0 : j0 + n], in_=y_bf[:]

from contextlib import ExitStack

import concourse.mybir as mybir

K, T, S, N, G, H = 512, 2048, 512, 512, 2048, 512
FLOPS = 2 * K * H * S + 2 * H * N * S

F32 = mybir.dt.float32
BF16 = mybir.dt.bfloat16
I32 = mybir.dt.int32
U32 = mybir.dt.uint32
U16 = mybir.dt.uint16
U8 = mybir.dt.uint8
FP8X4 = mybir.dt.float8_e4m3fn_x4
FP4X4 = mybir.dt.float4_e2m1fn_x4
ACT = mybir.ActivationFunctionType
ALU = mybir.AluOpType

P = 128
HALF = S // 2
CHUNK = 128
N1_ON_VECTOR = 4
Z_CHUNKS = [(j0, CHUNK) for j0 in range(0, S, CHUNK)]
OUT_CHUNKS = [(0, 128), (128, 256), (384, 128)]


def entries(lst, j0, n):
    return lst[:, j0 // 16 : (j0 + n) // 16]


def tile_picked_hpqhopmxsum_none_po_kernel(
    tc, x_words, x_scales, d_words, d_scales, gn, w1_words, w1_scales, offs, k1, n1, n2, n3, n4, out_0, out_1, out_2
):
    nc = tc.nc
    with ExitStack() as ctx:
        lists = ctx.enter_context(tc.tile_pool(name="lists", bufs=1))
        sb = ctx.enter_context(tc.tile_pool(name="sb", bufs=1))
        psum = ctx.enter_context(tc.psum_pool(name="psum", bufs=1))

        def load_list(name, src):
            lst = lists.tile([P, S // 16], U16, name=name)
            nc.sync.dma_start(lst[:], src)
            return lst

        def words_of(packed):
            return packed[0].rearrange("p n r -> p (n r)").bitcast(I32)

        k1_l = load_list("k1_l", k1)
        offs_l = load_list("offs_l", offs)
        gain = sb.tile([P, 4], F32)
        nc.sync.dma_start(gain[:], gn.rearrange("(p t) o -> p (t o)", t=4))
        n1_l = load_list("n1_l", n1)
        n2_l = load_list("n2_l", n2)

        planes = sb.tile([P, S + H + N], U8, align_bytes=64)
        nc.gpsimd.memset(planes[:, S + H :].bitcast(I32), 0)
        nc.scalar.dma_start(planes[0:P:8, S + H :].bitcast(I32), w1_scales[0].bitcast(I32))

        d_scale_tab = sb.tile([P, G], U8, align_bytes=64)
        x_scale_tab = sb.tile([P, T], U8, align_bytes=64)
        nc.vector.memset(d_scale_tab[:].bitcast(I32), 0)
        nc.gpsimd.memset(x_scale_tab[:].bitcast(I32), 0)
        nc.sync.dma_start(d_scale_tab[0:P:8, :].bitcast(I32), d_scales[0].bitcast(I32))
        nc.sync.dma_start(x_scale_tab[0:P:8, :].bitcast(I32), x_scales[0].bitcast(I32))

        d_tab = sb.tile([P, G], I32, align_bytes=64)
        nc.sync.dma_start(d_tab[:], words_of(d_words))
        x_tab = sb.tile([P, T], I32, tag="x_words_then_w1_dealt", align_bytes=64)
        nc.sync.dma_start(x_tab[:], words_of(x_words))
        w1_raw = sb.tile([P, 2 * N], U8, align_bytes=64)
        nc.sync.dma_start(w1_raw[:].bitcast(I32), w1_words[0].bitcast(I32))
        n3_l = load_list("n3_l", n3)
        n4_l = load_list("n4_l", n4)

        gain_abs = sb.tile([P, 4], F32)
        nc.scalar.activation(gain_abs[:], gain[:], ACT.Abs, scale=0.0625)
        widest = CHUNK
        gain_sign = sb.tile([P, widest, 4], BF16, align_bytes=64)
        nc.scalar.activation(gain_sign[:], gain[:].unsqueeze(1).to_broadcast([P, widest, 4]), ACT.Sign)

        d_scale_picked = sb.tile([P, H], U8, align_bytes=64)
        x_scale_picked = sb.tile([P, S], U8, align_bytes=64)
        nc.vector.tensor_copy(d_scale_picked[:], d_scale_tab[:].indirect(k1_l[:]))
        nc.vector.tensor_copy(x_scale_picked[:], x_scale_tab[:].indirect(offs_l[:]))
        nc.vector.tensor_copy(
            planes[:, S : S + H].rearrange("p (t m) -> p t m", t=4), d_scale_picked[:].rearrange("p (m t) -> p t m", t=4)
        )
        nc.vector.tensor_copy(planes[:, :S].bitcast(I32), x_scale_picked[:].bitcast(I32))
        for r in range(1, 4):
            nc.scalar.dma_start(planes[r:P:32, :].bitcast(I32), planes[8 * r : P : 32, :].bitcast(I32))

        d_picked = sb.tile([P, H], U32, align_bytes=64)
        nc.vector.tensor_copy(d_picked[:], d_tab[:].bitcast(U32).indirect(k1_l[:]))
        d_codes = sb.tile([P, H], U32, align_bytes=64)
        nc.vector.tensor_copy(
            d_codes[:].bitcast(I32).rearrange("p (t c i) -> p c t i", t=4, i=4),
            d_picked[:].bitcast(I32).rearrange("p (c i t) -> p c t i", t=4, i=4),
        )

        x_codes = [sb.tile([P, HALF], U32, name=f"x_codes{u}", align_bytes=64) for u in range(2)]
        for u in range(2):
            nc.vector.tensor_copy(x_codes[u][:], x_tab[:].bitcast(U32).indirect(entries(offs_l, u * HALF, HALF)))

        w1_dealt = sb.tile([P, 3 * N], U8, tag="x_words_then_w1_dealt", align_bytes=64)
        nc.vector.tensor_copy(
            w1_dealt[:, : 2 * N].rearrange("p (t m b) -> p t m b", t=4, b=2),
            w1_raw[:].rearrange("p (m t b) -> p t m b", t=4, b=2),
        )
        nc.vector.tensor_copy(
            w1_dealt[:, 2 * N :].rearrange("p (t m) -> p t m", t=4),
            planes[:, S + H :].rearrange("p (m t) -> p t m", t=4),
        )

        h = [sb.tile([P, S], F32, name=f"h{t}") for t in range(4)]
        for t, u in [(t, u) for t in range(4) for u in range(2)]:
            acc = psum.tile([P, HALF], F32, name="acc", tag=f"bank{2 * t + u}")
            nc.tensor.matmul_mx(
                out=acc[:],
                lhsT=d_codes[:, t * P : (t + 1) * P].bitcast(FP8X4),
                lhsT_scale=planes[:, S + t * P : S + (t + 1) * P],
                rhs=x_codes[u][:].bitcast(FP8X4),
                rhs_scale=planes[:, u * HALF : (u + 1) * HALF],
                start=True,
                stop=True,
            )
            nc.scalar.activation(h[t][:, u * HALF : (u + 1) * HALF], acc[:], ACT.Copy, scale=gain_abs[:, t : t + 1])

        st = sb.tile([P, 4, S], F32)
        for t in range(4):
            h_n1 = [sb.tile([P, HALF], F32, name=f"h_n1_{u}", tag=f"h_n1_{u}" if 2 * t + u < N1_ON_VECTOR else f"h_n1_{t}_{u}") for u in range(2)]
            for u in range(2):
                window = h[t][:].indirect(entries(n1_l, u * HALF, HALF))
                if 2 * t + u < N1_ON_VECTOR:
                    nc.vector.tensor_copy(h_n1[u][:], window)
                else:
                    nc.scalar.activation(h_n1[u][:], window, ACT.Copy)
            for u in range(2):
                cols = slice(u * HALF, (u + 1) * HALF)
                nc.vector.tensor_tensor(st[:, t, cols], h[t][:, cols], h_n1[u][:], ALU.subtract)

        st_n2 = [sb.tile([P, 4, CHUNK], F32, name=f"st_n2_{c}") for c in range(4)]
        for c, t in [(c, t) for c in range(4) for t in range(4)]:
            window = st[:, t, :].indirect(entries(n2_l, c * CHUNK, CHUNK))
            if c == 0 and t >= 2:
                nc.vector.tensor_copy(st_n2[c][:, t, :], window)
            else:
                nc.scalar.activation(st_n2[c][:, t, :], window, ACT.Copy)

        early = [psum.tile([P, 2 * CHUNK], F32, name="early", tag=f"bank{t}") for t in range(4)]
        late = [psum.tile([P, 2, CHUNK], F32, name="late", tag=f"bank{4 + b}") for b in range(4)]
        for c, (j0, n) in enumerate(Z_CHUNKS):
            z_abs = sb.tile([P, 4 * n], BF16, name=f"z_abs{c}", align_bytes=64)
            nc.vector.tensor_tensor(
                z_abs[:].rearrange("p (c i t) -> p c t i", t=4, i=2),
                st[:, :, j0 : j0 + n].rearrange("p t (c i) -> p c t i", i=2),
                st_n2[c][:].rearrange("p t (c i) -> p c t i", i=2),
                ALU.max,
            )
            z = sb.tile([P, 4 * n], BF16, name=f"z{c}", align_bytes=64)
            nc.vector.tensor_tensor(z[:], z_abs[:], gain_sign[:, :n, :].rearrange("p j t -> p (j t)"), ALU.mult)
            z_codes = sb.tile([P, n], U32, name=f"z_codes{c}", align_bytes=64)
            z_plane = sb.tile([P, n], U8, name=f"z_plane{c}", align_bytes=64)
            nc.vector.quantize_mx(out=z_codes[:].bitcast(FP8X4), scales=z_plane[:], in_=z[:])
            for t in range(4):
                nc.tensor.matmul_mx(
                    out=early[t][:, j0 : j0 + n] if c < 2 else late[2 * (c - 2) + t // 2][:, t % 2, :],
                    lhsT=w1_dealt[:, 2 * t * P : 2 * (t + 1) * P].bitcast(FP4X4),
                    lhsT_scale=w1_dealt[:, 2 * N + t * P : 2 * N + (t + 1) * P],
                    rhs=z_codes[:].bitcast(FP8X4),
                    rhs_scale=z_plane[:],
                    start=True,
                    stop=True,
                )

        h2 = [sb.tile([P, S], F32, name=f"h2_{t}") for t in range(4)]
        for t in range(4):
            nc.scalar.copy(h2[t][:, : 2 * CHUNK], early[t][:])
        for c in (2, 3):
            for t in range(4):
                src = late[2 * (c - 2) + t // 2][:, t % 2, :]
                if c == 3:
                    nc.vector.tensor_copy(h2[t][:, c * CHUNK : (c + 1) * CHUNK], src)
                else:
                    nc.scalar.copy(h2[t][:, c * CHUNK : (c + 1) * CHUNK], src)

        out_rows = out_0.rearrange("(p t) j -> p t j", t=4)
        out_codes = sb.tile([P, S], U32, align_bytes=64)
        out_plane = sb.tile([P, S], U8, align_bytes=64)
        for c, (j0, n) in enumerate(OUT_CHUNKS):
            h2_n4 = sb.tile([P, 4, n], F32, name=f"h2_n4_{c}")
            y = sb.tile([P, 4, n], F32, name=f"y{c}")
            for t in range(4):
                nc.scalar.activation(h2_n4[:, t, :], h2[t][:].indirect(entries(n4_l, j0, n)), ACT.Copy, scale=0.75)
                if c == 2 and t >= 1:
                    h2_n3 = sb.tile([P, n], F32, name=f"h2_n3_{t}")
                    nc.scalar.activation(h2_n3[:], h2[t][:].indirect(entries(n3_l, j0, n)), ACT.Copy)
                    nc.vector.tensor_tensor(y[:, t, :], h2_n3[:], h2_n4[:, t, :], ALU.add)
                else:
                    nc.vector.tensor_tensor(y[:, t, :], h2[t][:].indirect(entries(n3_l, j0, n)), h2_n4[:, t, :], ALU.add)
            nc.sync.dma_start(out_rows[:, :, j0 : j0 + n], y[:])
            y_bf = sb.tile([P, 4 * n], BF16, name=f"y_bf{c}", align_bytes=64)
            nc.vector.tensor_copy(
                y_bf[:].rearrange("p (c i t) -> p c t i", t=4, i=2), y[:].rearrange("p t (c i) -> p c t i", i=2)
            )
            nc.vector.quantize_mx(
                out=out_codes[:, j0 : j0 + n].bitcast(FP8X4), scales=out_plane[:, j0 : j0 + n], in_=y_bf[:]
            )
            nc.sync.dma_start(words_of(out_1)[:, j0 : j0 + n], out_codes[:, j0 : j0 + n].bitcast(I32))
        for q in range(4):
            queue = nc.scalar if q % 2 else nc.sync
            queue.dma_start(out_2[0, 4 * q : 4 * q + 4, :].bitcast(I32), out_plane[32 * q : 32 * q + 4, :].bitcast(I32))
